import numpy as np
import ml_dtypes


def mxq(x, axis, fmt="e4m3"):
    dtype, down = {"e4m3": (ml_dtypes.float8_e4m3fn, 7), "e5m2": (ml_dtypes.float8_e5m2, 14)}[fmt]
    v = np.moveaxis(np.asarray(x, np.float32).astype(ml_dtypes.bfloat16).astype(np.float64), axis, -1)
    blocks = v.reshape(v.shape[:-1] + (-1, 32))
    amax = np.abs(blocks).max(-1, keepdims=True)
    byte = np.maximum(np.where(amax > 0, np.frexp(amax)[1] - 1 + 127, 0) - down, 1)
    scale = np.exp2(byte - 127.0)
    codes = (blocks / scale).astype(np.float32).astype(dtype).astype(np.float64)
    return np.moveaxis((codes * scale).reshape(v.shape), -1, axis)


WIDE = False


def mx_kscale(k):
    if not WIDE:
        return np.ones(k)
    levels = np.array([10, -10, 5, -5, 0])
    if k % 512:
        return np.exp2(np.random.permutation(np.resize(levels, k // 32))).repeat(32)
    a = np.empty((k // 512, 16))
    for p in range(k // 512):
        a[p, :8] = np.random.permutation(np.resize(levels, 8))
        for g in range(8):
            far = levels[np.abs(levels - a[p, g]) >= 10]
            a[p, g + 8] = far[np.random.randint(len(far))]
    return np.exp2(a.ravel()).repeat(32)


def f64(x):
    return np.asarray(x).astype(np.float64)


def striped(idx):
    return np.tile(idx.reshape(-1, 16).T, (8, 1)).astype(np.uint16)


def unstriped(offs):
    return offs[:16].T.reshape(-1).astype(np.int64)


def pack_weight(w):
    k, n = w.shape
    w = f64(np.asarray(w, np.float32).astype(ml_dtypes.bfloat16)).reshape(k // 32, 32, n)
    amax = np.abs(w).max(1)
    byte = np.clip(np.where(amax > 0, np.frexp(amax)[1] - 1 + 127 - 7, 1), 1, 254)
    scaled = (w * np.exp2(127.0 - byte)[:, None, :]).reshape(k, n).astype(np.float32)
    words = np.ascontiguousarray(scaled.reshape(k // 512, 128, 4, n).transpose(0, 1, 3, 2)).astype(ml_dtypes.float8_e4m3fn).view(np.uint8)
    return words, np.ascontiguousarray(byte.astype(np.uint8).reshape(k // 512, 16, n))


def unpack_weight(words, scales):
    g, p, n, _ = words.shape
    vals = np.ascontiguousarray(words).view(ml_dtypes.float8_e4m3fn).astype(np.float64) * np.repeat(np.exp2(scales.astype(np.float64) - 127.0), 8, axis=1)[..., None]
    return vals.transpose(0, 1, 3, 2).reshape(g * 512, n)


def silu(v):
    return v / (1.0 + np.exp(-np.maximum(v, -700.0)))


K, T, S, D, N, H, V, W, U = 512, 2048, 1024, 4, 128, 512, 256, 4096, 512


def setup_inputs():
    n = np.random.standard_normal
    s = mx_kscale(K)[:, None]
    u = mx_kscale(H)
    packed_xT = pack_weight(n((K, T)) * s)
    packed_eT = pack_weight(n((K, W)) * s)
    return {
        "x_words": packed_xT[0],
        "x_scales": packed_xT[1],
        "w1": (n((K, H)) / np.sqrt(K) / s).astype(np.float32),
        "e_words": packed_eT[0],
        "e_scales": packed_eT[1],
        "w2": (n((K, H)) / np.sqrt(K) / s).astype(np.float32),
        "loc": (n((H, U))).astype(np.float32),
        "unit": (np.random.uniform(0.6, 1.4, (H, 1)) * u[:, None]).astype(np.float32),
        "w3": (n((H, N)) / np.sqrt(H) / u[:, None]).astype(np.float32),
        "offs": striped(np.random.permutation(T)[:S]),
        "ngr": striped(np.random.permutation(W)[:S]),
        "win": striped(np.random.permutation(np.concatenate([np.arange(V), np.random.randint(0, V, U - V)]))),
    }


def reference(x_words, x_scales, w1, e_words, e_scales, w2, loc, unit, w3, offs, ngr, win):
    xq = unpack_weight(x_words, x_scales)[:, unstriped(offs)]
    y = mxq(f64(w1), 0, "e4m3").T @ xq
    e_ngr = unpack_weight(e_words, e_scales)[:, unstriped(ngr)]
    ye = mxq(f64(w2), 0, "e4m3").T @ e_ngr
    bh = y + ye
    pt = bh.reshape(len(bh), -1, D).max(axis=2)
    dp = bh - np.repeat(pt, D, axis=1)
    ed = np.exp(1.5 * np.tanh(dp))
    soft = ed.reshape(len(ed), -1, D).mean(axis=2)
    sc = soft[:, unstriped(win)]
    zz2 = sc * pt[:, unstriped(win)] + f64(loc)
    hid = f64(unit) * silu(zz2)
    return mxq(f64(w3), 0, "e4m3").T @ mxq(hid, 0, "e4m3")

@@ -1,0 +1,327 @@
+from contextlib import ExitStack
+
+import concourse.mybir as mybir
+from concourse.masks import make_identity
+
+K, T, S, D, N, H, V, W, U = 512, 2048, 1024, 4, 128, 512, 256, 4096, 512
+FLOPS = 2 * (2 * K * H * S + H * N * U)
+
+F32 = mybir.dt.float32
+BF16 = mybir.dt.bfloat16
+I32 = mybir.dt.int32
+U32 = mybir.dt.uint32
+U16 = mybir.dt.uint16
+U8 = mybir.dt.uint8
+FP8X4 = mybir.dt.float8_e4m3fn_x4
+ALU = mybir.AluOpType
+ACT = mybir.ActivationFunctionType
+AXIS = mybir.AxisListType
+
+P = 128
+PACK = 4
+BANK = 512
+BLOCKS = H // P
+HALVES = S // BANK
+PATCHES = BANK // D
+WINDOW = 704
+E_PLANE = 4
+
+
+def tile_picked_ybltpt_silu_p_kernel(
+    tc, x_words, x_scales, w1, e_words, e_scales, w2, loc, unit, w3, offs, ngr, win, out
+):
+    nc = tc.nc
+    with ExitStack() as ctx:
+        lists = ctx.enter_context(tc.tile_pool(name="lists", bufs=1))
+        keep = ctx.enter_context(tc.tile_pool(name="keep", bufs=1))
+        work = ctx.enter_context(tc.tile_pool(name="work", bufs=3))
+        psum = ctx.enter_context(tc.psum_pool(name="psum", bufs=1))
+
+        offs_t = lists.tile([P, S // 16], U16)
+        ngr_t = lists.tile([P, S // 16], U16)
+        win_t = lists.tile([P, U // 16], U16)
+        xw_tab = keep.tile([P, T], U32)
+        ew_tab = keep.tile([P, W], U32)
+        xs_tab = keep.tile([P, T], U8)
+        es_tab = keep.tile([P, W], U8)
+        ident = keep.tile([P, P], F32)
+        unit_t = keep.tile([P, PACK], F32)
+        unit_row = keep.tile([P, H], F32)
+        loc_t = keep.tile([P, BLOCKS, U], F32)
+        w3_raw = keep.tile([P, PACK, N], F32)
+        w_raw = [[keep.tile([P, PACK, 2 * P], F32, name=f"w_raw{i}{a}") for a in range(2)] for i in range(2)]
+        q_win = [keep.tile([P, WINDOW], F32, name=f"q_win{b}") for b in range(BLOCKS)]
+
+        nc.vector.memset(xs_tab[:].bitcast(I32), 0)
+        nc.vector.memset(es_tab[:].bitcast(I32), 0)
+        for b in range(BLOCKS):
+            nc.vector.memset(q_win[b][:, V:], 0.0)
+
+        def load_scales(engine, table, scales, first):
+            rows = scales[0].bitcast(I32).rearrange("(q r) c -> r q c", r=PACK)
+            for r in range(PACK):
+                engine.dma_start(out=table[:].bitcast(I32)[first + r : P : 32, :], in_=rows[r])
+
+        def load_words(table, words):
+            nc.sync.dma_start(out=table[:].bitcast(I32), in_=words[0].rearrange("p n t -> p (n t)").bitcast(I32))
+
+        nc.sync.dma_start(offs_t[:], offs)
+        load_scales(nc.sync, xs_tab, x_scales, 0)
+        load_words(xw_tab, x_words)
+        nc.sync.dma_start(ngr_t[:], ngr)
+        load_scales(nc.gpsimd, es_tab, e_scales, E_PLANE)
+        nc.gpsimd.dma_start(out=unit_t[:], in_=unit.rearrange("(p t) o -> p (t o)", t=PACK))
+        make_identity(nc, ident[:])
+        for a in range(2):
+            for i, w in enumerate((w1, w2)):
+                nc.sync.dma_start(
+                    out=w_raw[i][a][:],
+                    in_=w.rearrange("(p j) c -> p j c", j=PACK)[:, :, a * 2 * P : (a + 1) * 2 * P],
+                )
+            if a == 0:
+                load_words(ew_tab, e_words)
+        nc.sync.dma_start(win_t[:], win)
+        nc.sync.dma_start(out=loc_t[:], in_=loc.rearrange("(b p) r -> p b r", p=P))
+        nc.sync.dma_start(out=w3_raw[:], in_=w3.rearrange("(p j) n -> p j n", j=PACK))
+
+        spread = psum.tile([P, PACK, P], F32, tag="z", bufs=2)
+        for t in range(PACK):
+            nc.tensor.transpose(spread[:, t, :], unit_t[:, t : t + 1].to_broadcast([P, P]), ident[:])
+        nc.scalar.copy(
+            out=unit_row[:].rearrange("q (p t) -> q p t", t=PACK), in_=spread[:].rearrange("q t p -> q p t")
+        )
+
+        xs_g = keep.tile([P, S], U8, align_bytes=64)
+        es_g = keep.tile([P, S], U8, align_bytes=64)
+        xw_g = [keep.tile([P, BANK], U32, name=f"xw_g{h}", align_bytes=64) for h in range(HALVES)]
+        ew_g = [keep.tile([P, BANK], U32, name=f"ew_g{h}", align_bytes=64) for h in range(HALVES)]
+        cols16 = BANK // 16
+        nc.vector.tensor_copy(xs_g[:], xs_tab[:].indirect(offs_t[:]))
+        for h in range(HALVES):
+            nc.vector.tensor_copy(xw_g[h][:], xw_tab[:].indirect(offs_t[:, h * cols16 : (h + 1) * cols16]))
+        nc.vector.tensor_copy(es_g[:], es_tab[:].indirect(ngr_t[:]))
+
+        def interleave(engine, dst, src):
+            dst = dst.rearrange("p (c i t) -> p c t i", i=4, t=PACK)
+            src = src.rearrange("p t (c i) -> p c t i", i=4)
+            if engine == "scalar":
+                nc.scalar.copy(out=dst, in_=src)
+            else:
+                nc.gpsimd.tensor_scalar(dst, src, 1.0, 0.0, ALU.mult, ALU.add)
+
+        w_codes = [keep.tile([P, 2 * P], U32, name=f"w_codes{b}", align_bytes=64) for b in range(BLOCKS)]
+        w_scales = [keep.tile([P, 2 * P], U8, name=f"w_scales{b}", align_bytes=64) for b in range(BLOCKS)]
+        w_bf = [keep.tile([P, 2 * PACK * P], BF16, name=f"w_bf{b}", align_bytes=64) for b in range(BLOCKS)]
+
+        def cast_weights(b):
+            for i in range(2):
+                interleave(
+                    "scalar" if b < 3 else "gpsimd",
+                    w_bf[b][:, i * PACK * P : (i + 1) * PACK * P],
+                    w_raw[i][b // 2][:, :, (b % 2) * P : (b % 2 + 1) * P],
+                )
+
+        def quantize_weights(b):
+            nc.vector.quantize_mx(out=w_codes[b][:].bitcast(FP8X4), scales=w_scales[b][:], in_=w_bf[b][:])
+
+        for b in range(BLOCKS):
+            cast_weights(b)
+        quantize_weights(0)
+        quantize_weights(1)
+        for h in range(HALVES):
+            nc.vector.tensor_copy(ew_g[h][:], ew_tab[:].indirect(ngr_t[:, h * cols16 : (h + 1) * cols16]))
+
+        w3_bf = keep.tile([P, PACK * N], BF16, align_bytes=64)
+        w3_codes = keep.tile([P, N], U32, align_bytes=64)
+        w3_scales = keep.tile([P, N], U8, align_bytes=64)
+        interleave("gpsimd", w3_bf[:], w3_raw[:])
+
+        units = [(b, h) for b in range(BLOCKS) for h in range(HALVES)]
+        last = len(units) - 1
+        pt = [keep.tile([P, V], F32, name=f"pt{b}") for b in range(BLOCKS)]
+        bh, dp, th, ed, sums_t, sums_sb, sums, qg, z = {}, {}, {}, {}, {}, {}, {}, {}, {}
+
+        def product(u):
+            b, h = units[u]
+            cols = slice(h * BANK, (h + 1) * BANK)
+            bh[u] = psum.tile([P, BANK], F32, tag="bh", bufs=3, name="bh")
+            nc.tensor.matmul_mx(
+                out=bh[u][:], lhsT=w_codes[b][:, 0:P].bitcast(FP8X4), lhsT_scale=w_scales[b][:, 0:P],
+                rhs=xw_g[h][:].bitcast(FP8X4), rhs_scale=xs_g[:, cols], start=True, stop=False,
+            )
+            nc.tensor.matmul_mx(
+                out=bh[u][:], lhsT=w_codes[b][:, P : 2 * P].bitcast(FP8X4), lhsT_scale=w_scales[b][:, P : 2 * P],
+                rhs=ew_g[h][:].bitcast(FP8X4), rhs_scale=es_g[E_PLANE:P, cols], start=False, stop=True,
+            )
+
+        def pt_part(u):
+            b, h = units[u]
+            return pt[b][:, h * PATCHES : (h + 1) * PATCHES]
+
+        def patch_max(u):
+            nc.vector.tensor_reduce(
+                out=pt_part(u), in_=bh[u][:].rearrange("p (v d) -> p v d", d=D), axis=AXIS.X, op=ALU.max
+            )
+
+        def difference(u):
+            dp[u] = work.tile([P, BANK], F32, tag="dp", name="dp")
+            if u == last:
+                nc.vector.tensor_tensor(
+                    dp[u][:].rearrange("p (v d) -> p v d", d=D),
+                    bh[u][:].rearrange("p (v d) -> p v d", d=D),
+                    pt_part(u).unsqueeze(2).to_broadcast([P, PATCHES, D]),
+                    ALU.subtract,
+                )
+            else:
+                nc.vector.tensor_tensor(
+                    dp[u][:].rearrange("p (d v) -> p d v", d=D),
+                    bh[u][:].rearrange("p (v d) -> p d v", d=D),
+                    pt_part(u).unsqueeze(1).to_broadcast([P, D, PATCHES]),
+                    ALU.subtract,
+                )
+
+        def squash(u):
+            if u == last:
+                th[u] = keep.tile([P, BANK], F32, tag="act", name="th_last")
+            else:
+                th[u] = work.tile([P, BANK], F32, tag="th", name="th")
+            nc.scalar.activation(th[u][:], dp[u][:], ACT.Tanh)
+
+        def grow(u):
+            ed[u] = work.tile([P, BANK], F32, tag="ed", name="ed")
+            nc.scalar.activation(ed[u][:], th[u][:], ACT.Exp, scale=1.5)
+
+        def sum_turned(u):
+            sums_t[u] = psum.tile([P, P], F32, tag="st", bufs=2, name="sums_t")
+            for d in range(D):
+                nc.tensor.matmul(
+                    sums_t[u][:], ed[u][:, d * PATCHES : (d + 1) * PATCHES], ident[:],
+                    start=(d == 0), stop=(d == D - 1), is_transpose=True,
+                )
+
+        def sum_out(u):
+            sums_sb[u] = work.tile([P, P], F32, tag="sums_sb", name="sums_sb")
+            nc.scalar.copy(out=sums_sb[u][:], in_=sums_t[u][:])
+
+        def sum_back(u):
+            b, h = units[u]
+            if h == 0:
+                sums[b] = psum.tile([P, V], F32, tag="sb", bufs=1, name="sums")
+            nc.tensor.transpose(sums[b][:, h * PATCHES : (h + 1) * PATCHES], sums_sb[u][:], ident[:])
+
+        def patch_value(b):
+            width = V if b < BLOCKS - 1 else PATCHES
+            nc.vector.scalar_tensor_tensor(
+                q_win[b][:, 0:width], sums[b][:, 0:width], 1.0 / D, pt[b][:, 0:width], ALU.mult, ALU.mult
+            )
+
+        def last_patch_value():
+            total = keep.tile([P, PATCHES], F32)
+            nc.vector.tensor_reduce(
+                out=total[:], in_=ed[last][:].rearrange("p (v d) -> p v d", d=D), axis=AXIS.X, op=ALU.add
+            )
+            nc.vector.scalar_tensor_tensor(
+                q_win[BLOCKS - 1][:, PATCHES:V], total[:], 1.0 / D, pt_part(last), ALU.mult, ALU.mult
+            )
+
+        HALF = U // 2
+
+        def look_up(b, g):
+            if b < BLOCKS - 1:
+                if g == 0:
+                    qg[b] = keep.tile([P, U], F32, name=f"qg{b}")
+                    nc.vector.tensor_copy(qg[b][:], q_win[b][:].indirect(win_t[:]))
+                qg[b, g] = qg[b][:, g * HALF : (g + 1) * HALF]
+            else:
+                qg[b, g] = keep.tile([P, HALF], F32, name=f"qg{b}{g}")[:]
+                nc.vector.tensor_copy(qg[b, g], q_win[b][:].indirect(win_t[:, g * HALF // 16 : (g + 1) * HALF // 16]))
+
+        def add_local(b, g):
+            if b == BLOCKS - 1:
+                tag, bufs = (("bh", 3), ("sb", 1))[g]
+                z[b, g] = psum.tile([P, 2, P], F32, tag=tag, bufs=bufs, name="z")[:]
+            else:
+                if g == 0:
+                    tag, bufs = ("z", 2) if b < 2 else ("bh", 3)
+                    z[b] = psum.tile([P, U // P, P], F32, tag=tag, bufs=bufs, name="z")
+                z[b, g] = z[b][:, 2 * g : 2 * g + 2, :]
+            for c in range(2):
+                place = z[b, g][:, c, :]
+                r0 = g * HALF + c * P
+                nc.tensor.matmul(place, loc_t[:, b, r0 : r0 + P], ident[:], start=True, stop=False, is_transpose=True)
+                nc.tensor.matmul(
+                    place, qg[b, g][:, c * P : (c + 1) * P], ident[:], start=False, stop=True, is_transpose=True
+                )
+
+        product(0)
+        product(1)
+        patch_max(0)
+        for u in range(len(units) + 2):
+            if u + 2 <= last:
+                if u % 2 == 0 and u > 0:
+                    quantize_weights(u // 2 + 1)
+                product(u + 2)
+            if u + 1 <= last:
+                patch_max(u + 1)
+            if u <= last:
+                difference(u)
+                squash(u)
+            if 1 <= u <= last + 1:
+                grow(u - 1)
+                if u - 1 < last:
+                    sum_turned(u - 1)
+            if 2 <= u and u - 2 < last:
+                sum_out(u - 2)
+                sum_back(u - 2)
+        nc.vector.quantize_mx(out=w3_codes[:].bitcast(FP8X4), scales=w3_scales[:], in_=w3_bf[:])
+        for b in range(BLOCKS):
+            patch_value(b)
+            if b == BLOCKS - 1:
+                last_patch_value()
+            for g in range(2):
+                look_up(b, g)
+                add_local(b, g)
+
+        clock = keep.tile([P, 16], F32)
+        nc.gpsimd.tensor_copy(clock[:, 0:1], ed[last][:, 0:1])
+        nc.gpsimd.tensor_copy(clock[:, 8:9], qg[3, 1][:, 0:1])
+        act = keep.tile([P, BLOCKS * U], F32, tag="act", name="act")
+        hid_t = [keep.tile([P, 2, H], BF16, name=f"hid_t{g}") for g in range(2)]
+        for b in range(BLOCKS):
+            if b < BLOCKS - 1:
+                nc.scalar.activation(
+                    act[:, b * U : (b + 1) * U], z[b][:].rearrange("p c f -> p (c f)"), ACT.Silu
+                )
+            for g in range(2):
+                part = act[:, b * U + g * HALF : b * U + (g + 1) * HALF].rearrange("p (c f) -> p c f", c=2)
+                if b == BLOCKS - 1:
+                    nc.scalar.activation(part, z[b, g], ACT.Silu)
+                nc.vector.tensor_tensor(
+                    hid_t[g][:, :, b * P : (b + 1) * P],
+                    part,
+                    unit_row[:, b * P : (b + 1) * P].unsqueeze(1).to_broadcast([P, 2, P]),
+                    ALU.mult,
+                )
+
+        for g in range(2):
+            turned = psum.tile([P, 2, 2, P], F32, tag="z", bufs=2, name="turned")
+            for c in range(2):
+                words = hid_t[g][:, c, :].bitcast(F32)
+                for e in range(2):
+                    nc.tensor.transpose(turned[:, c, e, :], words[:, e : H // 2 : 2], ident[:])
+            hid = keep.tile([P, HALF * PACK], BF16, name=f"hid{g}", align_bytes=64)
+            nc.scalar.copy(
+                out=hid[:].bitcast(F32).rearrange("p (c r e) -> p c r e", c=2, e=2),
+                in_=turned[:].rearrange("p c e r -> p c r e"),
+            )
+            hid_codes = keep.tile([P, HALF], U32, name=f"hid_codes{g}", align_bytes=64)
+            hid_scales = keep.tile([P, HALF], U8, name=f"hid_scales{g}", align_bytes=64)
+            nc.vector.quantize_mx(out=hid_codes[:].bitcast(FP8X4), scales=hid_scales[:], in_=hid[:])
+            acc = psum.tile([P, HALF], F32, tag="st", bufs=2, name="acc")
+            nc.tensor.matmul_mx(
+                out=acc[:], lhsT=w3_codes[:].bitcast(FP8X4), lhsT_scale=w3_scales[:],
+                rhs=hid_codes[:].bitcast(FP8X4), rhs_scale=hid_scales[:], start=True, stop=True,
+            )
+            result = keep.tile([P, HALF], F32, name=f"result{g}")
+            nc.scalar.copy(out=result[:], in_=acc[:])
+            nc.sync.dma_start(out=out[:, g * HALF : (g + 1) * HALF], in_=result[:])

@@ -49,13 +49,16 @@ def tile_picked_ybltpt_silu_p_kernel(
         unit_row = keep.tile([P, H], F32)
         loc_t = keep.tile([P, BLOCKS, U], F32)
         w3_raw = keep.tile([P, PACK, N], F32)
-        w_raw = [[keep.tile([P, PACK, 2 * P], F32, name=f"w_raw{i}{a}") for a in range(2)] for i in range(2)]
-        q_win = [keep.tile([P, WINDOW], F32, name=f"q_win{b}") for b in range(BLOCKS)]
+        w_parts = ((0, 1), (1, 2), (2, 4))
+        w_raw = [
+            [keep.tile([P, PACK, (hi - lo) * P], F32, name=f"w_raw{i}{lo}") for lo, hi in w_parts] for i in range(2)
+        ]
+        q_all = keep.tile([P, (BLOCKS - 1) * V + WINDOW], F32)
+        q_win = [q_all[:, (BLOCKS - 1 - b) * V : (BLOCKS - 1 - b) * V + WINDOW] for b in range(BLOCKS)]
 
         nc.vector.memset(xs_tab[:].bitcast(I32), 0)
         nc.vector.memset(es_tab[:].bitcast(I32), 0)
-        for b in range(BLOCKS):
-            nc.vector.memset(q_win[b][:, V:], 0.0)
+        nc.gpsimd.memset(q_win[0][:, V:], 0.0)
 
         def load_scales(engine, table, scales, first):
             rows = scales[0].bitcast(I32).rearrange("(q r) c -> r q c", r=PACK)
@@ -65,31 +68,28 @@ def tile_picked_ybltpt_silu_p_kernel(
         def load_words(table, words):
             nc.sync.dma_start(out=table[:].bitcast(I32), in_=words[0].rearrange("p n t -> p (n t)").bitcast(I32))
 
+        def load_weights(i, a):
+            lo, hi = w_parts[a]
+            nc.sync.dma_start(
+                out=w_raw[i][a][:], in_=(w1, w2)[i].rearrange("(p j) c -> p j c", j=PACK)[:, :, lo * P : hi * P]
+            )
+
+        make_identity(nc, ident[:])
         nc.sync.dma_start(offs_t[:], offs)
         load_scales(nc.sync, xs_tab, x_scales, 0)
         load_words(xw_tab, x_words)
         nc.sync.dma_start(ngr_t[:], ngr)
-        load_scales(nc.gpsimd, es_tab, e_scales, E_PLANE)
-        nc.gpsimd.dma_start(out=unit_t[:], in_=unit.rearrange("(p t) o -> p (t o)", t=PACK))
-        make_identity(nc, ident[:])
-        for a in range(2):
-            for i, w in enumerate((w1, w2)):
-                nc.sync.dma_start(
-                    out=w_raw[i][a][:],
-                    in_=w.rearrange("(p j) c -> p j c", j=PACK)[:, :, a * 2 * P : (a + 1) * 2 * P],
-                )
-            if a == 0:
-                load_words(ew_tab, e_words)
+        load_weights(0, 0)
+        load_scales(nc.sync, es_tab, e_scales, E_PLANE)
+        load_words(ew_tab, e_words)
+        load_weights(1, 0)
+        nc.sync.dma_start(out=unit_t[:], in_=unit.rearrange("(p t) o -> p (t o)", t=PACK))
+        for a in range(1, 3):
+            for i in range(2):
+                load_weights(i, a)
         nc.sync.dma_start(win_t[:], win)
         nc.sync.dma_start(out=loc_t[:], in_=loc.rearrange("(b p) r -> p b r", p=P))
         nc.sync.dma_start(out=w3_raw[:], in_=w3.rearrange("(p j) n -> p j n", j=PACK))
-
-        spread = psum.tile([P, PACK, P], F32, tag="z", bufs=2)
-        for t in range(PACK):
-            nc.tensor.transpose(spread[:, t, :], unit_t[:, t : t + 1].to_broadcast([P, P]), ident[:])
-        nc.scalar.copy(
-            out=unit_row[:].rearrange("q (p t) -> q p t", t=PACK), in_=spread[:].rearrange("q t p -> q p t")
-        )
 
         xs_g = keep.tile([P, S], U8, align_bytes=64)
         es_g = keep.tile([P, S], U8, align_bytes=64)
@@ -116,18 +116,30 @@ def tile_picked_ybltpt_silu_p_kernel(
         def cast_weights(b):
             for i in range(2):
                 interleave(
-                    "scalar" if b < 3 else "gpsimd",
+                    "scalar" if b < 2 or i == 0 else "gpsimd",
                     w_bf[b][:, i * PACK * P : (i + 1) * PACK * P],
-                    w_raw[i][b // 2][:, :, (b % 2) * P : (b % 2 + 1) * P],
+                    w_raw[i][min(b, 2)][:, :, max(b - 2, 0) * P : (max(b - 2, 0) + 1) * P],
                 )
 
         def quantize_weights(b):
             nc.vector.quantize_mx(out=w_codes[b][:].bitcast(FP8X4), scales=w_scales[b][:], in_=w_bf[b][:])
 
-        for b in range(BLOCKS):
+        cast_weights(0)
+        spread = psum.tile([P, PACK, P], F32, tag="sb", bufs=2)
+        for t in range(PACK):
+            nc.tensor.transpose(spread[:, t, :], unit_t[:, t : t + 1].to_broadcast([P, P]), ident[:])
+        nc.scalar.copy(
+            out=unit_row[:].rearrange("q (p t) -> q p t", t=PACK), in_=spread[:].rearrange("q t p -> q p t")
+        )
+
+        for b in range(1, BLOCKS):
             cast_weights(b)
-        quantize_weights(0)
-        quantize_weights(1)
+        for i in range(2):
+            nc.vector.quantize_mx(
+                out=w_codes[0][:, i * P : (i + 1) * P].bitcast(FP8X4),
+                scales=w_scales[0][:, i * P : (i + 1) * P],
+                in_=w_bf[0][:, i * PACK * P : (i + 1) * PACK * P],
+            )
         for h in range(HALVES):
             nc.vector.tensor_copy(ew_g[h][:], ew_tab[:].indirect(ngr_t[:, h * cols16 : (h + 1) * cols16]))
 
@@ -144,7 +156,7 @@ def tile_picked_ybltpt_silu_p_kernel(
         def product(u):
             b, h = units[u]
             cols = slice(h * BANK, (h + 1) * BANK)
-            bh[u] = psum.tile([P, BANK], F32, tag="bh", bufs=3, name="bh")
+            bh[u] = psum.tile([P, BANK], F32, tag="bh", bufs=4, name="bh")
             nc.tensor.matmul_mx(
                 out=bh[u][:], lhsT=w_codes[b][:, 0:P].bitcast(FP8X4), lhsT_scale=w_scales[b][:, 0:P],
                 rhs=xw_g[h][:].bitcast(FP8X4), rhs_scale=xs_g[:, cols], start=True, stop=False,
@@ -164,25 +176,19 @@ def tile_picked_ybltpt_silu_p_kernel(
             )
 
         def difference(u):
-            dp[u] = work.tile([P, BANK], F32, tag="dp", name="dp")
-            if u == last:
-                nc.vector.tensor_tensor(
-                    dp[u][:].rearrange("p (v d) -> p v d", d=D),
-                    bh[u][:].rearrange("p (v d) -> p v d", d=D),
-                    pt_part(u).unsqueeze(2).to_broadcast([P, PATCHES, D]),
-                    ALU.subtract,
-                )
-            else:
-                nc.vector.tensor_tensor(
-                    dp[u][:].rearrange("p (d v) -> p d v", d=D),
-                    bh[u][:].rearrange("p (v d) -> p d v", d=D),
-                    pt_part(u).unsqueeze(1).to_broadcast([P, D, PATCHES]),
-                    ALU.subtract,
-                )
+            dp[u] = keep.tile([P, BANK], F32, tag=f"dp{u}", name="dp")
+            nc.vector.tensor_tensor(
+                dp[u][:].rearrange("p (d v) -> p d v", d=D),
+                bh[u][:].rearrange("p (v d) -> p d v", d=D),
+                pt_part(u).unsqueeze(1).to_broadcast([P, D, PATCHES]),
+                ALU.subtract,
+            )
 
         def squash(u):
             if u == last:
                 th[u] = keep.tile([P, BANK], F32, tag="act", name="th_last")
+            elif u == last - 1:
+                th[u] = keep.tile([P, BANK], F32, tag="th6", name="th_6")
             else:
                 th[u] = work.tile([P, BANK], F32, tag="th", name="th")
             nc.scalar.activation(th[u][:], dp[u][:], ACT.Tanh)
@@ -201,64 +207,53 @@ def tile_picked_ybltpt_silu_p_kernel(
 
         def sum_out(u):
             sums_sb[u] = work.tile([P, P], F32, tag="sums_sb", name="sums_sb")
-            nc.scalar.copy(out=sums_sb[u][:], in_=sums_t[u][:])
+            if u == last:
+                nc.vector.tensor_copy(out=sums_sb[u][:], in_=sums_t[u][:])
+            else:
+                nc.scalar.copy(out=sums_sb[u][:], in_=sums_t[u][:])
 
         def sum_back(u):
             b, h = units[u]
             if h == 0:
-                sums[b] = psum.tile([P, V], F32, tag="sb", bufs=1, name="sums")
+                sums[b] = psum.tile([P, V], F32, tag="sb", bufs=2, name="sums")
             nc.tensor.transpose(sums[b][:, h * PATCHES : (h + 1) * PATCHES], sums_sb[u][:], ident[:])
 
         def patch_value(b):
-            width = V if b < BLOCKS - 1 else PATCHES
-            nc.vector.scalar_tensor_tensor(
-                q_win[b][:, 0:width], sums[b][:, 0:width], 1.0 / D, pt[b][:, 0:width], ALU.mult, ALU.mult
-            )
+            nc.vector.scalar_tensor_tensor(q_win[b][:, 0:V], sums[b][:], 1.0 / D, pt[b][:], ALU.mult, ALU.mult)
 
-        def last_patch_value():
-            total = keep.tile([P, PATCHES], F32)
-            nc.vector.tensor_reduce(
-                out=total[:], in_=ed[last][:].rearrange("p (v d) -> p v d", d=D), axis=AXIS.X, op=ALU.add
-            )
-            nc.vector.scalar_tensor_tensor(
-                q_win[BLOCKS - 1][:, PATCHES:V], total[:], 1.0 / D, pt_part(last), ALU.mult, ALU.mult
-            )
+        groups = ((0, 2), (2, 3), (3, 4))
 
-        HALF = U // 2
+        def look_up(b):
+            qg[b] = keep.tile([P, U], F32, tag=("dp6", "dp7", "th6")[b], name=f"qg{b}")
+            nc.vector.tensor_copy(qg[b][:], q_win[b].indirect(win_t[:]))
+            z[b] = psum.tile([P, U // P, P], F32, tag="bh", bufs=4, name="z")
+            add_local(b, z[b], qg[b], 0, U // P)
 
-        def look_up(b, g):
-            if b < BLOCKS - 1:
-                if g == 0:
-                    qg[b] = keep.tile([P, U], F32, name=f"qg{b}")
-                    nc.vector.tensor_copy(qg[b][:], q_win[b][:].indirect(win_t[:]))
-                qg[b, g] = qg[b][:, g * HALF : (g + 1) * HALF]
-            else:
-                qg[b, g] = keep.tile([P, HALF], F32, name=f"qg{b}{g}")[:]
-                nc.vector.tensor_copy(qg[b, g], q_win[b][:].indirect(win_t[:, g * HALF // 16 : (g + 1) * HALF // 16]))
+        def look_up_last(g):
+            lo, hi = groups[g]
+            b = BLOCKS - 1
+            qg[b, g] = keep.tile([P, (hi - lo) * P], F32, name=f"qg{b}{g}")
+            nc.vector.tensor_copy(qg[b, g][:], q_win[b].indirect(win_t[:, lo * P // 16 : hi * P // 16]))
+            tag, bufs = ("bh", 4) if g == 0 else ("st", 2)
+            z[b, g] = psum.tile([P, hi - lo, P], F32, tag=tag, bufs=bufs, name="z")
+            add_local(b, z[b, g], qg[b, g], lo, hi)
 
-        def add_local(b, g):
-            if b == BLOCKS - 1:
-                tag, bufs = (("bh", 3), ("sb", 1))[g]
-                z[b, g] = psum.tile([P, 2, P], F32, tag=tag, bufs=bufs, name="z")[:]
-            else:
-                if g == 0:
-                    tag, bufs = ("z", 2) if b < 2 else ("bh", 3)
-                    z[b] = psum.tile([P, U // P, P], F32, tag=tag, bufs=bufs, name="z")
-                z[b, g] = z[b][:, 2 * g : 2 * g + 2, :]
-            for c in range(2):
-                place = z[b, g][:, c, :]
-                r0 = g * HALF + c * P
-                nc.tensor.matmul(place, loc_t[:, b, r0 : r0 + P], ident[:], start=True, stop=False, is_transpose=True)
+        def add_local(b, bank, values, lo, hi):
+            for c in range(lo, hi):
+                place = bank[:, c - lo, :]
                 nc.tensor.matmul(
-                    place, qg[b, g][:, c * P : (c + 1) * P], ident[:], start=False, stop=True, is_transpose=True
+                    place, loc_t[:, b, c * P : (c + 1) * P], ident[:], start=True, stop=False, is_transpose=True
+                )
+                nc.tensor.matmul(
+                    place, values[:, (c - lo) * P : (c - lo + 1) * P], ident[:], start=False, stop=True, is_transpose=True
                 )
 
         product(0)
         product(1)
         patch_max(0)
-        for u in range(len(units) + 2):
+        for u in range(len(units) + 1):
             if u + 2 <= last:
-                if u % 2 == 0 and u > 0:
+                if u % 2 == 0:
                     quantize_weights(u // 2 + 1)
                 product(u + 2)
             if u + 1 <= last:
@@ -266,62 +261,63 @@ def tile_picked_ybltpt_silu_p_kernel(
             if u <= last:
                 difference(u)
                 squash(u)
-            if 1 <= u <= last + 1:
+            if 1 <= u:
                 grow(u - 1)
-                if u - 1 < last:
-                    sum_turned(u - 1)
-            if 2 <= u and u - 2 < last:
+                sum_turned(u - 1)
+            if 2 <= u:
                 sum_out(u - 2)
                 sum_back(u - 2)
+                if u % 2 == 1:
+                    patch_value((u - 2) // 2)
         nc.vector.quantize_mx(out=w3_codes[:].bitcast(FP8X4), scales=w3_scales[:], in_=w3_bf[:])
-        for b in range(BLOCKS):
-            patch_value(b)
-            if b == BLOCKS - 1:
-                last_patch_value()
-            for g in range(2):
-                look_up(b, g)
-                add_local(b, g)
+        look_up(0)
+        look_up(1)
+        sum_out(last)
+        sum_back(last)
+        look_up(2)
+        patch_value(BLOCKS - 1)
+        for g in range(len(groups)):
+            look_up_last(g)
 
         clock = keep.tile([P, 16], F32)
         nc.gpsimd.tensor_copy(clock[:, 0:1], ed[last][:, 0:1])
-        nc.gpsimd.tensor_copy(clock[:, 8:9], qg[3, 1][:, 0:1])
+        nc.gpsimd.tensor_copy(clock[:, 8:9], qg[3, 2][:, 0:1])
         act = keep.tile([P, BLOCKS * U], F32, tag="act", name="act")
-        hid_t = [keep.tile([P, 2, H], BF16, name=f"hid_t{g}") for g in range(2)]
-        for b in range(BLOCKS):
-            if b < BLOCKS - 1:
-                nc.scalar.activation(
-                    act[:, b * U : (b + 1) * U], z[b][:].rearrange("p c f -> p (c f)"), ACT.Silu
-                )
-            for g in range(2):
-                part = act[:, b * U + g * HALF : b * U + (g + 1) * HALF].rearrange("p (c f) -> p c f", c=2)
+        hid_t = [keep.tile([P, hi - lo, H], BF16, name=f"hid_t{lo}") for lo, hi in groups]
+        for b in range(BLOCKS - 1):
+            nc.scalar.activation(act[:, b * U : (b + 1) * U], z[b][:].rearrange("p c f -> p (c f)"), ACT.Silu)
+        for g, (lo, hi) in enumerate(groups):
+            for b in range(BLOCKS):
+                part = act[:, b * U + lo * P : b * U + hi * P].rearrange("p (c f) -> p c f", f=P)
                 if b == BLOCKS - 1:
-                    nc.scalar.activation(part, z[b, g], ACT.Silu)
+                    nc.scalar.activation(part, z[b, g][:], ACT.Silu)
                 nc.vector.tensor_tensor(
                     hid_t[g][:, :, b * P : (b + 1) * P],
                     part,
-                    unit_row[:, b * P : (b + 1) * P].unsqueeze(1).to_broadcast([P, 2, P]),
+                    unit_row[:, b * P : (b + 1) * P].unsqueeze(1).to_broadcast([P, hi - lo, P]),
                     ALU.mult,
                 )
 
-        for g in range(2):
-            turned = psum.tile([P, 2, 2, P], F32, tag="z", bufs=2, name="turned")
-            for c in range(2):
+        for g, (lo, hi) in enumerate(groups):
+            width = (hi - lo) * P
+            turned = psum.tile([P, hi - lo, 2, P], F32, tag="bh", bufs=4, name="turned")
+            for c in range(hi - lo):
                 words = hid_t[g][:, c, :].bitcast(F32)
                 for e in range(2):
                     nc.tensor.transpose(turned[:, c, e, :], words[:, e : H // 2 : 2], ident[:])
-            hid = keep.tile([P, HALF * PACK], BF16, name=f"hid{g}", align_bytes=64)
+            hid = keep.tile([P, width * PACK], BF16, name=f"hid{g}", align_bytes=64)
             nc.scalar.copy(
-                out=hid[:].bitcast(F32).rearrange("p (c r e) -> p c r e", c=2, e=2),
+                out=hid[:].bitcast(F32).rearrange("p (c r e) -> p c r e", r=P, e=2),
                 in_=turned[:].rearrange("p c e r -> p c r e"),
             )
-            hid_codes = keep.tile([P, HALF], U32, name=f"hid_codes{g}", align_bytes=64)
-            hid_scales = keep.tile([P, HALF], U8, name=f"hid_scales{g}", align_bytes=64)
+            hid_codes = keep.tile([P, width], U32, name=f"hid_codes{g}", align_bytes=64)
+            hid_scales = keep.tile([P, width], U8, name=f"hid_scales{g}", align_bytes=64)
             nc.vector.quantize_mx(out=hid_codes[:].bitcast(FP8X4), scales=hid_scales[:], in_=hid[:])
-            acc = psum.tile([P, HALF], F32, tag="st", bufs=2, name="acc")
+            acc = psum.tile([P, width], F32, tag="sb", bufs=2, name="acc")
             nc.tensor.matmul_mx(
                 out=acc[:], lhsT=w3_codes[:].bitcast(FP8X4), lhsT_scale=w3_scales[:],
                 rhs=hid_codes[:].bitcast(FP8X4), rhs_scale=hid_scales[:], start=True, stop=True,
             )
-            result = keep.tile([P, HALF], F32, name=f"result{g}")
+            result = keep.tile([P, width], F32, name=f"result{g}")
             nc.scalar.copy(out=result[:], in_=acc[:])
-            nc.sync.dma_start(out=out[:, g * HALF : (g + 1) * HALF], in_=result[:])
+            nc.sync.dma_start(out=out[:, lo * P : hi * P], in_=result[:])

@@ -1,3 +1,4 @@
+import math
 from contextlib import ExitStack
 
 import concourse.mybir as mybir
@@ -25,6 +26,7 @@ HALVES = S // BANK
 PATCHES = BANK // D
 WINDOW = 704
 E_PLANE = 4
+POOL_UNITS = 2
 
 
 def tile_picked_ybltpt_silu_p_kernel(
@@ -34,7 +36,7 @@ def tile_picked_ybltpt_silu_p_kernel(
     with ExitStack() as ctx:
         lists = ctx.enter_context(tc.tile_pool(name="lists", bufs=1))
         keep = ctx.enter_context(tc.tile_pool(name="keep", bufs=1))
-        work = ctx.enter_context(tc.tile_pool(name="work", bufs=3))
+        work = ctx.enter_context(tc.tile_pool(name="work", bufs=4))
         psum = ctx.enter_context(tc.psum_pool(name="psum", bufs=1))
 
         offs_t = lists.tile([P, S // 16], U16)
@@ -45,18 +47,18 @@ def tile_picked_ybltpt_silu_p_kernel(
         xs_tab = keep.tile([P, T], U8)
         es_tab = keep.tile([P, W], U8)
         ident = keep.tile([P, P], F32)
-        unit_t = keep.tile([P, PACK], F32)
         unit_row = keep.tile([P, H], F32)
         loc_t = keep.tile([P, BLOCKS, U], F32)
         w3_raw = keep.tile([P, PACK, N], F32)
-        w_parts = ((0, 1), (1, 2), (2, 4))
+        w_parts = ((0, 2), (2, 4))
         w_raw = [
             [keep.tile([P, PACK, (hi - lo) * P], F32, name=f"w_raw{i}{lo}") for lo, hi in w_parts] for i in range(2)
         ]
         q_all = keep.tile([P, (BLOCKS - 1) * V + WINDOW], F32)
         q_win = [q_all[:, (BLOCKS - 1 - b) * V : (BLOCKS - 1 - b) * V + WINDOW] for b in range(BLOCKS)]
 
-        nc.vector.memset(xs_tab[:].bitcast(I32), 0)
+        nc.vector.memset(xs_tab[:, 0 : T // 2].bitcast(I32), 0)
+        nc.gpsimd.memset(xs_tab[:, T // 2 : T].bitcast(I32), 0)
         nc.vector.memset(es_tab[:].bitcast(I32), 0)
         nc.gpsimd.memset(q_win[0][:, V:], 0.0)
 
@@ -76,20 +78,19 @@ def tile_picked_ybltpt_silu_p_kernel(
 
         make_identity(nc, ident[:])
         nc.sync.dma_start(offs_t[:], offs)
+        nc.sync.dma_start(ngr_t[:], ngr)
+        nc.sync.dma_start(win_t[:], win)
         load_scales(nc.sync, xs_tab, x_scales, 0)
         load_words(xw_tab, x_words)
-        nc.sync.dma_start(ngr_t[:], ngr)
         load_weights(0, 0)
         load_scales(nc.sync, es_tab, e_scales, E_PLANE)
-        load_words(ew_tab, e_words)
         load_weights(1, 0)
-        nc.sync.dma_start(out=unit_t[:], in_=unit.rearrange("(p t) o -> p (t o)", t=PACK))
-        for a in range(1, 3):
-            for i in range(2):
-                load_weights(i, a)
-        nc.sync.dma_start(win_t[:], win)
+        load_words(ew_tab, e_words)
+        for i in range(2):
+            load_weights(i, 1)
         nc.sync.dma_start(out=loc_t[:], in_=loc.rearrange("(b p) r -> p b r", p=P))
         nc.sync.dma_start(out=w3_raw[:], in_=w3.rearrange("(p j) n -> p j n", j=PACK))
+        nc.sync.dma_start(out=unit_row[:], in_=unit.rearrange("f o -> (f o)").partition_broadcast(P))
 
         xs_g = keep.tile([P, S], U8, align_bytes=64)
         es_g = keep.tile([P, S], U8, align_bytes=64)
@@ -116,37 +117,25 @@ def tile_picked_ybltpt_silu_p_kernel(
         def cast_weights(b):
             for i in range(2):
                 interleave(
-                    "scalar" if b < 2 or i == 0 else "gpsimd",
+                    "scalar",
                     w_bf[b][:, i * PACK * P : (i + 1) * PACK * P],
-                    w_raw[i][min(b, 2)][:, :, max(b - 2, 0) * P : (max(b - 2, 0) + 1) * P],
+                    w_raw[i][b // 2][:, :, (b % 2) * P : (b % 2 + 1) * P],
                 )
 
         def quantize_weights(b):
             nc.vector.quantize_mx(out=w_codes[b][:].bitcast(FP8X4), scales=w_scales[b][:], in_=w_bf[b][:])
 
         cast_weights(0)
-        spread = psum.tile([P, PACK, P], F32, tag="sb", bufs=2)
-        for t in range(PACK):
-            nc.tensor.transpose(spread[:, t, :], unit_t[:, t : t + 1].to_broadcast([P, P]), ident[:])
-        nc.scalar.copy(
-            out=unit_row[:].rearrange("q (p t) -> q p t", t=PACK), in_=spread[:].rearrange("q t p -> q p t")
-        )
-
         for b in range(1, BLOCKS):
             cast_weights(b)
-        for i in range(2):
-            nc.vector.quantize_mx(
-                out=w_codes[0][:, i * P : (i + 1) * P].bitcast(FP8X4),
-                scales=w_scales[0][:, i * P : (i + 1) * P],
-                in_=w_bf[0][:, i * PACK * P : (i + 1) * PACK * P],
-            )
+        quantize_weights(0)
+        quantize_weights(1)
         for h in range(HALVES):
             nc.vector.tensor_copy(ew_g[h][:], ew_tab[:].indirect(ngr_t[:, h * cols16 : (h + 1) * cols16]))
 
         w3_bf = keep.tile([P, PACK * N], BF16, align_bytes=64)
         w3_codes = keep.tile([P, N], U32, align_bytes=64)
         w3_scales = keep.tile([P, N], U8, align_bytes=64)
-        interleave("gpsimd", w3_bf[:], w3_raw[:])
 
         units = [(b, h) for b in range(BLOCKS) for h in range(HALVES)]
         last = len(units) - 1
@@ -187,15 +176,13 @@ def tile_picked_ybltpt_silu_p_kernel(
         def squash(u):
             if u == last:
                 th[u] = keep.tile([P, BANK], F32, tag="act", name="th_last")
-            elif u == last - 1:
-                th[u] = keep.tile([P, BANK], F32, tag="th6", name="th_6")
             else:
                 th[u] = work.tile([P, BANK], F32, tag="th", name="th")
             nc.scalar.activation(th[u][:], dp[u][:], ACT.Tanh)
 
         def grow(u):
-            ed[u] = work.tile([P, BANK], F32, tag="ed", name="ed")
-            nc.scalar.activation(ed[u][:], th[u][:], ACT.Exp, scale=1.5)
+            ed[u] = keep.tile([P, BANK], F32, tag=f"ed{u}", name="ed")
+            nc.scalar.activation(ed[u][:], th[u][:], ACT.Exp, scale=1.5, bias=-math.log(D))
 
         def sum_turned(u):
             sums_t[u] = psum.tile([P, P], F32, tag="st", bufs=2, name="sums_t")
@@ -219,14 +206,30 @@ def tile_picked_ybltpt_silu_p_kernel(
             nc.tensor.transpose(sums[b][:, h * PATCHES : (h + 1) * PATCHES], sums_sb[u][:], ident[:])
 
         def patch_value(b):
-            nc.vector.scalar_tensor_tensor(q_win[b][:, 0:V], sums[b][:], 1.0 / D, pt[b][:], ALU.mult, ALU.mult)
+            nc.vector.tensor_tensor(q_win[b][:, 0:V], sums[b][:], pt[b][:], ALU.mult)
+
+        def sum_on_gpsimd(u):
+            b, h = units[u]
+            pairs = work.tile([P, 2 * PATCHES], F32, tag="pairs", name="pairs")
+            total = work.tile([P, PATCHES], F32, tag="total", name="total")
+            nc.gpsimd.tensor_tensor(pairs[:], ed[u][:, 0 : 2 * PATCHES], ed[u][:, 2 * PATCHES : BANK], ALU.add)
+            nc.gpsimd.tensor_tensor(total[:], pairs[:, 0:PATCHES], pairs[:, PATCHES : 2 * PATCHES], ALU.add)
+            nc.gpsimd.tensor_tensor(q_win[b][:, h * PATCHES : (h + 1) * PATCHES], total[:], pt_part(u), ALU.mult)
 
         groups = ((0, 2), (2, 3), (3, 4))
 
         def look_up(b):
-            qg[b] = keep.tile([P, U], F32, tag=("dp6", "dp7", "th6")[b], name=f"qg{b}")
-            nc.vector.tensor_copy(qg[b][:], q_win[b].indirect(win_t[:]))
-            z[b] = psum.tile([P, U // P, P], F32, tag="bh", bufs=4, name="z")
+            if b == 0:
+                qg["pair"] = keep.tile([P, 2 * U], F32, tag="dp5", name="qg_pair")
+            if b < 2:
+                qg[b] = qg["pair"][:, b * U : (b + 1) * U]
+            else:
+                qg[b] = keep.tile([P, U], F32, tag="ed7", name="qg_third")[:]
+            nc.vector.tensor_copy(qg[b], q_win[b].indirect(win_t[:]))
+
+        def add_block(b):
+            tag, bufs = ("st", 2) if b < 2 else ("bh", 4)
+            z[b] = psum.tile([P, U // P, P], F32, tag=tag, bufs=bufs, name="z")
             add_local(b, z[b], qg[b], 0, U // P)
 
         def look_up_last(g):
@@ -234,7 +237,7 @@ def tile_picked_ybltpt_silu_p_kernel(
             b = BLOCKS - 1
             qg[b, g] = keep.tile([P, (hi - lo) * P], F32, name=f"qg{b}{g}")
             nc.vector.tensor_copy(qg[b, g][:], q_win[b].indirect(win_t[:, lo * P // 16 : hi * P // 16]))
-            tag, bufs = ("bh", 4) if g == 0 else ("st", 2)
+            tag, bufs = ("bh", 4)
             z[b, g] = psum.tile([P, hi - lo, P], F32, tag=tag, bufs=bufs, name="z")
             add_local(b, z[b, g], qg[b, g], lo, hi)
 
@@ -253,7 +256,7 @@ def tile_picked_ybltpt_silu_p_kernel(
         patch_max(0)
         for u in range(len(units) + 1):
             if u + 2 <= last:
-                if u % 2 == 0:
+                if u % 2 == 0 and u > 0:
                     quantize_weights(u // 2 + 1)
                 product(u + 2)
             if u + 1 <= last:
@@ -263,25 +266,29 @@ def tile_picked_ybltpt_silu_p_kernel(
                 squash(u)
             if 1 <= u:
                 grow(u - 1)
-                sum_turned(u - 1)
-            if 2 <= u:
+                if u - 1 < POOL_UNITS:
+                    sum_on_gpsimd(u - 1)
+                else:
+                    sum_turned(u - 1)
+            if 2 + POOL_UNITS <= u:
                 sum_out(u - 2)
                 sum_back(u - 2)
                 if u % 2 == 1:
                     patch_value((u - 2) // 2)
-        nc.vector.quantize_mx(out=w3_codes[:].bitcast(FP8X4), scales=w3_scales[:], in_=w3_bf[:])
+        interleave("gpsimd", w3_bf[:], w3_raw[:])
         look_up(0)
+        add_block(0)
         look_up(1)
         sum_out(last)
         sum_back(last)
+        add_block(1)
         look_up(2)
+        add_block(2)
         patch_value(BLOCKS - 1)
         for g in range(len(groups)):
             look_up_last(g)
 
-        clock = keep.tile([P, 16], F32)
-        nc.gpsimd.tensor_copy(clock[:, 0:1], ed[last][:, 0:1])
-        nc.gpsimd.tensor_copy(clock[:, 8:9], qg[3, 2][:, 0:1])
+        nc.vector.quantize_mx(out=w3_codes[:].bitcast(FP8X4), scales=w3_scales[:], in_=w3_bf[:])
         act = keep.tile([P, BLOCKS * U], F32, tag="act", name="act")
         hid_t = [keep.tile([P, hi - lo, H], BF16, name=f"hid_t{lo}") for lo, hi in groups]
         for b in range(BLOCKS - 1):
@@ -291,7 +298,7 @@ def tile_picked_ybltpt_silu_p_kernel(
                 part = act[:, b * U + lo * P : b * U + hi * P].rearrange("p (c f) -> p c f", f=P)
                 if b == BLOCKS - 1:
                     nc.scalar.activation(part, z[b, g][:], ACT.Silu)
-                nc.vector.tensor_tensor(
+                (nc.gpsimd if b == 0 else nc.vector).tensor_tensor(
                     hid_t[g][:, :, b * P : (b + 1) * P],
                     part,
                     unit_row[:, b * P : (b + 1) * P].unsqueeze(1).to_broadcast([P, hi - lo, P]),
@@ -300,7 +307,8 @@ def tile_picked_ybltpt_silu_p_kernel(
 
         for g, (lo, hi) in enumerate(groups):
             width = (hi - lo) * P
-            turned = psum.tile([P, hi - lo, 2, P], F32, tag="bh", bufs=4, name="turned")
+            tag, bufs = ("st", 2) if g < 2 else ("bh", 4)
+            turned = psum.tile([P, hi - lo, 2, P], F32, tag=tag, bufs=bufs, name="turned")
             for c in range(hi - lo):
                 words = hid_t[g][:, c, :].bitcast(F32)
                 for e in range(2):
@@ -313,11 +321,12 @@ def tile_picked_ybltpt_silu_p_kernel(
             hid_codes = keep.tile([P, width], U32, name=f"hid_codes{g}", align_bytes=64)
             hid_scales = keep.tile([P, width], U8, name=f"hid_scales{g}", align_bytes=64)
             nc.vector.quantize_mx(out=hid_codes[:].bitcast(FP8X4), scales=hid_scales[:], in_=hid[:])
-            acc = psum.tile([P, width], F32, tag="sb", bufs=2, name="acc")
+            tag, bufs = ("sb", 2) if g < 2 else ("bh", 4)
+            acc = psum.tile([P, width], F32, tag=tag, bufs=bufs, name="acc")
             nc.tensor.matmul_mx(
                 out=acc[:], lhsT=w3_codes[:].bitcast(FP8X4), lhsT_scale=w3_scales[:],
                 rhs=hid_codes[:].bitcast(FP8X4), rhs_scale=hid_scales[:], start=True, stop=True,
             )
             result = keep.tile([P, width], F32, name=f"result{g}")
-            nc.scalar.copy(out=result[:], in_=acc[:])
+            (nc.scalar.copy if g == 0 else nc.vector.tensor_copy)(out=result[:], in_=acc[:])
             nc.sync.dma_start(out=out[:, lo * P : hi * P], in_=result[:])

import math
from contextlib import ExitStack

import concourse.mybir as mybir
from concourse.masks import make_identity

K, T, S, D, N, H, V, W, U = 512, 2048, 1024, 4, 128, 512, 256, 4096, 512
FLOPS = 2 * (2 * K * H * S + H * N * U)

F32 = mybir.dt.float32
BF16 = mybir.dt.bfloat16
I32 = mybir.dt.int32
U32 = mybir.dt.uint32
U16 = mybir.dt.uint16
U8 = mybir.dt.uint8
FP8X4 = mybir.dt.float8_e4m3fn_x4
ALU = mybir.AluOpType
ACT = mybir.ActivationFunctionType
AXIS = mybir.AxisListType

P = 128
PACK = 4
BANK = 512
BLOCKS = H // P
HALVES = S // BANK
PATCHES = BANK // D
WINDOW = 704
E_PLANE = 4
POOL_UNITS = 2


def tile_picked_ybltpt_silu_p_kernel(
    tc, x_words, x_scales, w1, e_words, e_scales, w2, loc, unit, w3, offs, ngr, win, out
):
    nc = tc.nc
    with ExitStack() as ctx:
        lists = ctx.enter_context(tc.tile_pool(name="lists", bufs=1))
        keep = ctx.enter_context(tc.tile_pool(name="keep", bufs=1))
        work = ctx.enter_context(tc.tile_pool(name="work", bufs=4))
        psum = ctx.enter_context(tc.psum_pool(name="psum", bufs=1))

        offs_t = lists.tile([P, S // 16], U16)
        ngr_t = lists.tile([P, S // 16], U16)
        win_t = lists.tile([P, U // 16], U16)
        xw_tab = keep.tile([P, T], U32)
        ew_tab = keep.tile([P, W], U32)
        xs_tab = keep.tile([P, T], U8)
        es_tab = keep.tile([P, W], U8)
        ident = keep.tile([P, P], F32)
        unit_row = keep.tile([P, H], F32)
        loc_t = keep.tile([P, BLOCKS, U], F32)
        w3_raw = keep.tile([P, PACK, N], F32)
        w_parts = ((0, 2), (2, 4))
        w_raw = [
            [keep.tile([P, PACK, (hi - lo) * P], F32, name=f"w_raw{i}{lo}") for lo, hi in w_parts] for i in range(2)
        ]
        q_all = keep.tile([P, (BLOCKS - 1) * V + WINDOW], F32)
        q_win = [q_all[:, (BLOCKS - 1 - b) * V : (BLOCKS - 1 - b) * V + WINDOW] for b in range(BLOCKS)]

        nc.vector.memset(xs_tab[:, 0 : T // 2].bitcast(I32), 0)
        nc.gpsimd.memset(xs_tab[:, T // 2 : T].bitcast(I32), 0)
        nc.vector.memset(es_tab[:].bitcast(I32), 0)
        nc.gpsimd.memset(q_win[0][:, V:], 0.0)

        def load_scales(engine, table, scales, first):
            rows = scales[0].bitcast(I32).rearrange("(q r) c -> r q c", r=PACK)
            for r in range(PACK):
                engine.dma_start(out=table[:].bitcast(I32)[first + r : P : 32, :], in_=rows[r])

        def load_words(table, words):
            nc.sync.dma_start(out=table[:].bitcast(I32), in_=words[0].rearrange("p n t -> p (n t)").bitcast(I32))

        def load_weights(i, a):
            lo, hi = w_parts[a]
            nc.sync.dma_start(
                out=w_raw[i][a][:], in_=(w1, w2)[i].rearrange("(p j) c -> p j c", j=PACK)[:, :, lo * P : hi * P]
            )

        make_identity(nc, ident[:])
        nc.sync.dma_start(offs_t[:], offs)
        nc.sync.dma_start(ngr_t[:], ngr)
        nc.sync.dma_start(win_t[:], win)
        load_scales(nc.sync, xs_tab, x_scales, 0)
        load_words(xw_tab, x_words)
        load_weights(0, 0)
        load_scales(nc.sync, es_tab, e_scales, E_PLANE)
        load_weights(1, 0)
        load_words(ew_tab, e_words)
        for i in range(2):
            load_weights(i, 1)
        nc.sync.dma_start(out=loc_t[:], in_=loc.rearrange("(b p) r -> p b r", p=P))
        nc.sync.dma_start(out=w3_raw[:], in_=w3.rearrange("(p j) n -> p j n", j=PACK))
        nc.sync.dma_start(out=unit_row[:], in_=unit.rearrange("f o -> (f o)").partition_broadcast(P))

        xs_g = keep.tile([P, S], U8, align_bytes=64)
        es_g = keep.tile([P, S], U8, align_bytes=64)
        xw_g = [keep.tile([P, BANK], U32, name=f"xw_g{h}", align_bytes=64) for h in range(HALVES)]
        ew_g = [keep.tile([P, BANK], U32, name=f"ew_g{h}", align_bytes=64) for h in range(HALVES)]
        cols16 = BANK // 16
        nc.vector.tensor_copy(xs_g[:], xs_tab[:].indirect(offs_t[:]))
        for h in range(HALVES):
            nc.vector.tensor_copy(xw_g[h][:], xw_tab[:].indirect(offs_t[:, h * cols16 : (h + 1) * cols16]))
        nc.vector.tensor_copy(es_g[:], es_tab[:].indirect(ngr_t[:]))

        def interleave(engine, dst, src):
            dst = dst.rearrange("p (c i t) -> p c t i", i=4, t=PACK)
            src = src.rearrange("p t (c i) -> p c t i", i=4)
            if engine == "scalar":
                nc.scalar.copy(out=dst, in_=src)
            else:
                nc.gpsimd.tensor_scalar(dst, src, 1.0, 0.0, ALU.mult, ALU.add)

        w_codes = [keep.tile([P, 2 * P], U32, name=f"w_codes{b}", align_bytes=64) for b in range(BLOCKS)]
        w_scales = [keep.tile([P, 2 * P], U8, name=f"w_scales{b}", align_bytes=64) for b in range(BLOCKS)]
        w_bf = [keep.tile([P, 2 * PACK * P], BF16, name=f"w_bf{b}", align_bytes=64) for b in range(BLOCKS)]

        def cast_weights(b):
            for i in range(2):
                interleave(
                    "scalar",
                    w_bf[b][:, i * PACK * P : (i + 1) * PACK * P],
                    w_raw[i][b // 2][:, :, (b % 2) * P : (b % 2 + 1) * P],
                )

        def quantize_weights(b):
            nc.vector.quantize_mx(out=w_codes[b][:].bitcast(FP8X4), scales=w_scales[b][:], in_=w_bf[b][:])

        cast_weights(0)
        for b in range(1, BLOCKS):
            cast_weights(b)
        quantize_weights(0)
        quantize_weights(1)
        for h in range(HALVES):
            nc.vector.tensor_copy(ew_g[h][:], ew_tab[:].indirect(ngr_t[:, h * cols16 : (h + 1) * cols16]))

        w3_bf = keep.tile([P, PACK * N], BF16, align_bytes=64)
        w3_codes = keep.tile([P, N], U32, align_bytes=64)
        w3_scales = keep.tile([P, N], U8, align_bytes=64)

        units = [(b, h) for b in range(BLOCKS) for h in range(HALVES)]
        last = len(units) - 1
        pt = [keep.tile([P, V], F32, name=f"pt{b}") for b in range(BLOCKS)]
        bh, dp, th, ed, sums_t, sums_sb, sums, qg, z = {}, {}, {}, {}, {}, {}, {}, {}, {}

        def product(u):
            b, h = units[u]
            cols = slice(h * BANK, (h + 1) * BANK)
            bh[u] = psum.tile([P, BANK], F32, tag="bh", bufs=4, name="bh")
            nc.tensor.matmul_mx(
                out=bh[u][:], lhsT=w_codes[b][:, 0:P].bitcast(FP8X4), lhsT_scale=w_scales[b][:, 0:P],
                rhs=xw_g[h][:].bitcast(FP8X4), rhs_scale=xs_g[:, cols], start=True, stop=False,
            )
            nc.tensor.matmul_mx(
                out=bh[u][:], lhsT=w_codes[b][:, P : 2 * P].bitcast(FP8X4), lhsT_scale=w_scales[b][:, P : 2 * P],
                rhs=ew_g[h][:].bitcast(FP8X4), rhs_scale=es_g[E_PLANE:P, cols], start=False, stop=True,
            )

        def pt_part(u):
            b, h = units[u]
            return pt[b][:, h * PATCHES : (h + 1) * PATCHES]

        def patch_max(u):
            nc.vector.tensor_reduce(
                out=pt_part(u), in_=bh[u][:].rearrange("p (v d) -> p v d", d=D), axis=AXIS.X, op=ALU.max
            )

        def difference(u):
            dp[u] = keep.tile([P, BANK], F32, tag=f"dp{u}", name="dp")
            nc.vector.tensor_tensor(
                dp[u][:].rearrange("p (d v) -> p d v", d=D),
                bh[u][:].rearrange("p (v d) -> p d v", d=D),
                pt_part(u).unsqueeze(1).to_broadcast([P, D, PATCHES]),
                ALU.subtract,
            )

        def squash(u):
            if u == last:
                th[u] = keep.tile([P, BANK], F32, tag="act", name="th_last")
            else:
                th[u] = work.tile([P, BANK], F32, tag="th", name="th")
            nc.scalar.activation(th[u][:], dp[u][:], ACT.Tanh)

        def grow(u):
            ed[u] = keep.tile([P, BANK], F32, tag=f"ed{u}", name="ed")
            nc.scalar.activation(ed[u][:], th[u][:], ACT.Exp, scale=1.5, bias=-math.log(D))

        def sum_turned(u):
            sums_t[u] = psum.tile([P, P], F32, tag="st", bufs=2, name="sums_t")
            for d in range(D):
                nc.tensor.matmul(
                    sums_t[u][:], ed[u][:, d * PATCHES : (d + 1) * PATCHES], ident[:],
                    start=(d == 0), stop=(d == D - 1), is_transpose=True,
                )

        def sum_out(u):
            sums_sb[u] = work.tile([P, P], F32, tag="sums_sb", name="sums_sb")
            if u == last:
                nc.vector.tensor_copy(out=sums_sb[u][:], in_=sums_t[u][:])
            else:
                nc.scalar.copy(out=sums_sb[u][:], in_=sums_t[u][:])

        def sum_back(u):
            b, h = units[u]
            if h == 0:
                sums[b] = psum.tile([P, V], F32, tag="sb", bufs=2, name="sums")
            nc.tensor.transpose(sums[b][:, h * PATCHES : (h + 1) * PATCHES], sums_sb[u][:], ident[:])

        def patch_value(b):
            nc.vector.tensor_tensor(q_win[b][:, 0:V], sums[b][:], pt[b][:], ALU.mult)

        def sum_on_gpsimd(u):
            b, h = units[u]
            pairs = work.tile([P, 2 * PATCHES], F32, tag="pairs", name="pairs")
            total = work.tile([P, PATCHES], F32, tag="total", name="total")
            nc.gpsimd.tensor_tensor(pairs[:], ed[u][:, 0 : 2 * PATCHES], ed[u][:, 2 * PATCHES : BANK], ALU.add)
            nc.gpsimd.tensor_tensor(total[:], pairs[:, 0:PATCHES], pairs[:, PATCHES : 2 * PATCHES], ALU.add)
            nc.gpsimd.tensor_tensor(q_win[b][:, h * PATCHES : (h + 1) * PATCHES], total[:], pt_part(u), ALU.mult)

        groups = ((0, 2), (2, 3), (3, 4))

        def look_up(b):
            if b == 0:
                qg["pair"] = keep.tile([P, 2 * U], F32, tag="dp5", name="qg_pair")
            if b < 2:
                qg[b] = qg["pair"][:, b * U : (b + 1) * U]
            else:
                qg[b] = keep.tile([P, U], F32, tag="ed7", name="qg_third")[:]
            nc.vector.tensor_copy(qg[b], q_win[b].indirect(win_t[:]))

        def add_block(b):
            tag, bufs = ("st", 2) if b < 2 else ("bh", 4)
            z[b] = psum.tile([P, U // P, P], F32, tag=tag, bufs=bufs, name="z")
            add_local(b, z[b], qg[b], 0, U // P)

        def look_up_last(g):
            lo, hi = groups[g]
            b = BLOCKS - 1
            qg[b, g] = keep.tile([P, (hi - lo) * P], F32, name=f"qg{b}{g}")
            nc.vector.tensor_copy(qg[b, g][:], q_win[b].indirect(win_t[:, lo * P // 16 : hi * P // 16]))
            tag, bufs = ("bh", 4)
            z[b, g] = psum.tile([P, hi - lo, P], F32, tag=tag, bufs=bufs, name="z")
            add_local(b, z[b, g], qg[b, g], lo, hi)

        def add_local(b, bank, values, lo, hi):
            for c in range(lo, hi):
                place = bank[:, c - lo, :]
                nc.tensor.matmul(
                    place, loc_t[:, b, c * P : (c + 1) * P], ident[:], start=True, stop=False, is_transpose=True
                )
                nc.tensor.matmul(
                    place, values[:, (c - lo) * P : (c - lo + 1) * P], ident[:], start=False, stop=True, is_transpose=True
                )

        product(0)
        product(1)
        patch_max(0)
        for u in range(len(units) + 1):
            if u + 2 <= last:
                if u % 2 == 0 and u > 0:
                    quantize_weights(u // 2 + 1)
                product(u + 2)
            if u + 1 <= last:
                patch_max(u + 1)
            if u <= last:
                difference(u)
                squash(u)
            if 1 <= u:
                grow(u - 1)
                if u - 1 < POOL_UNITS:
                    sum_on_gpsimd(u - 1)
                else:
                    sum_turned(u - 1)
            if 2 + POOL_UNITS <= u:
                sum_out(u - 2)
                sum_back(u - 2)
                if u % 2 == 1:
                    patch_value((u - 2) // 2)
        interleave("gpsimd", w3_bf[:], w3_raw[:])
        look_up(0)
        add_block(0)
        look_up(1)
        sum_out(last)
        sum_back(last)
        add_block(1)
        look_up(2)
        add_block(2)
        patch_value(BLOCKS - 1)
        for g in range(len(groups)):
            look_up_last(g)

        nc.vector.quantize_mx(out=w3_codes[:].bitcast(FP8X4), scales=w3_scales[:], in_=w3_bf[:])
        act = keep.tile([P, BLOCKS * U], F32, tag="act", name="act")
        hid_t = [keep.tile([P, hi - lo, H], BF16, name=f"hid_t{lo}") for lo, hi in groups]
        for b in range(BLOCKS - 1):
            nc.scalar.activation(act[:, b * U : (b + 1) * U], z[b][:].rearrange("p c f -> p (c f)"), ACT.Silu)
        for g, (lo, hi) in enumerate(groups):
            for b in range(BLOCKS):
                part = act[:, b * U + lo * P : b * U + hi * P].rearrange("p (c f) -> p c f", f=P)
                if b == BLOCKS - 1:
                    nc.scalar.activation(part, z[b, g][:], ACT.Silu)
                (nc.gpsimd if b == 0 else nc.vector).tensor_tensor(
                    hid_t[g][:, :, b * P : (b + 1) * P],
                    part,
                    unit_row[:, b * P : (b + 1) * P].unsqueeze(1).to_broadcast([P, hi - lo, P]),
                    ALU.mult,
                )

        for g, (lo, hi) in enumerate(groups):
            width = (hi - lo) * P
            tag, bufs = ("st", 2) if g < 2 else ("bh", 4)
            turned = psum.tile([P, hi - lo, 2, P], F32, tag=tag, bufs=bufs, name="turned")
            for c in range(hi - lo):
                words = hid_t[g][:, c, :].bitcast(F32)
                for e in range(2):
                    nc.tensor.transpose(turned[:, c, e, :], words[:, e : H // 2 : 2], ident[:])
            hid = keep.tile([P, width * PACK], BF16, name=f"hid{g}", align_bytes=64)
            nc.scalar.copy(
                out=hid[:].bitcast(F32).rearrange("p (c r e) -> p c r e", r=P, e=2),
                in_=turned[:].rearrange("p c e r -> p c r e"),
            )
            hid_codes = keep.tile([P, width], U32, name=f"hid_codes{g}", align_bytes=64)
            hid_scales = keep.tile([P, width], U8, name=f"hid_scales{g}", align_bytes=64)
            nc.vector.quantize_mx(out=hid_codes[:].bitcast(FP8X4), scales=hid_scales[:], in_=hid[:])
            tag, bufs = ("sb", 2) if g < 2 else ("bh", 4)
            acc = psum.tile([P, width], F32, tag=tag, bufs=bufs, name="acc")
            nc.tensor.matmul_mx(
                out=acc[:], lhsT=w3_codes[:].bitcast(FP8X4), lhsT_scale=w3_scales[:],
                rhs=hid_codes[:].bitcast(FP8X4), rhs_scale=hid_scales[:], start=True, stop=True,
            )
            result = keep.tile([P, width], F32, name=f"result{g}")
            (nc.scalar.copy if g == 0 else nc.vector.tensor_copy)(out=result[:], in_=acc[:])
            nc.sync.dma_start(out=out[:, lo * P : hi * P], in_=result[:])
